import numpy as np
import ml_dtypes


def mxq(x, axis, fmt="e4m3"):
    dtype, down = {"e4m3": (ml_dtypes.float8_e4m3fn, 7), "e5m2": (ml_dtypes.float8_e5m2, 14)}[fmt]
    v = np.moveaxis(np.asarray(x, np.float32).astype(ml_dtypes.bfloat16).astype(np.float64), axis, -1)
    blocks = v.reshape(v.shape[:-1] + (-1, 32))
    amax = np.abs(blocks).max(-1, keepdims=True)
    byte = np.maximum(np.where(amax > 0, np.frexp(amax)[1] - 1 + 127, 0) - down, 1)
    scale = np.exp2(byte - 127.0)
    codes = (blocks / scale).astype(np.float32).astype(dtype).astype(np.float64)
    return np.moveaxis((codes * scale).reshape(v.shape), -1, axis)


WIDE = False


def mx_kscale(k):
    if not WIDE:
        return np.ones(k)
    levels = np.array([10, -10, 5, -5, 0])
    if k % 512:
        return np.exp2(np.random.permutation(np.resize(levels, k // 32))).repeat(32)
    a = np.empty((k // 512, 16))
    for p in range(k // 512):
        a[p, :8] = np.random.permutation(np.resize(levels, 8))
        for g in range(8):
            far = levels[np.abs(levels - a[p, g]) >= 10]
            a[p, g + 8] = far[np.random.randint(len(far))]
    return np.exp2(a.ravel()).repeat(32)


def f64(x):
    return np.asarray(x).astype(np.float64)


def striped8(idx):
    return np.asarray(idx).reshape(8, -1, 16).transpose(0, 2, 1).reshape(128, -1).astype(np.uint16)


def unstriped8(offs):
    return offs.reshape(8, 16, -1).transpose(0, 2, 1).reshape(8, -1).astype(np.int64)


def pick8(x, idx, run):
    r = np.arange(len(x))
    return x[r[:, None], idx[r % (8 * run) // run]]


E2M1 = np.array([0.0, 0.5, 1.0, 1.5, 2.0, 3.0, 4.0, 6.0, -0.0, -0.5, -1.0, -1.5, -2.0, -3.0, -4.0, -6.0])


def pack_weight(w, fmt):
    k, n = w.shape
    w = f64(np.asarray(w, np.float32).astype(ml_dtypes.bfloat16)).reshape(k // 32, 32, n)
    amax = np.abs(w).max(1)
    if fmt == "e4m3":
        byte = np.frexp(amax)[1] - 1 + 127 - 7
    else:
        mant, ex = np.frexp(amax / 6.0)
        byte = np.where(mant > 0.5, ex, ex - 1) + 127
    byte = np.clip(np.where(amax > 0, byte, 1), 1, 254)
    scaled = (w * np.exp2(127.0 - byte)[:, None, :]).reshape(k, n).astype(np.float32)
    by_word = np.ascontiguousarray(scaled.reshape(k // 512, 128, 4, n).transpose(0, 1, 3, 2))
    if fmt == "e4m3":
        words = by_word.astype(ml_dtypes.float8_e4m3fn).view(np.uint8)
    else:
        c = by_word.astype(ml_dtypes.float4_e2m1fn).view(np.uint8) & 0xF
        words = (c[..., 0::2] | (c[..., 1::2] << 4)).reshape(k // 512, 128, 2 * n)
    return np.ascontiguousarray(words), np.ascontiguousarray(byte.astype(np.uint8).reshape(k // 512, 16, n))


def unpack_weight(words, scales, fmt):
    g, _, n = scales.shape
    words = np.ascontiguousarray(words).reshape(g, 128, n, -1)
    if fmt == "e4m3":
        vals = words.view(ml_dtypes.float8_e4m3fn).astype(np.float64)
    else:
        nib = np.empty((g, 128, n, 4), np.uint8)
        nib[..., 0::2] = words & 0xF
        nib[..., 1::2] = words >> 4
        vals = E2M1[nib]
    vals = vals * np.repeat(np.exp2(scales.astype(np.float64) - 127.0), 8, axis=1)[..., None]
    return vals.transpose(0, 1, 3, 2).reshape(g * 512, n)


D, V, Q, I = 512, 2048, 128, 512


def setup_inputs():
    n = np.random.standard_normal
    idx = np.stack([np.random.permutation(V)[:I] for _ in range(8)])
    fd = mx_kscale(D)
    vocp = pack_weight(n((D, V)) / fd[:, None], "e2m1")
    return {
        "hid": (n((D, Q)) * 1.0 / np.sqrt(D) * fd[:, None]).astype(np.float32),
        "voc_words": vocp[0],
        "voc_scales": vocp[1],
        "aim": (np.random.uniform(4.0, 5.5, (Q, 1))).astype(np.float32),
        "dhid": (n((D, Q)) * 1.0 / np.sqrt(D) * fd[:, None]).astype(np.float32),
        "base": (0.5 * n((Q, V))).astype(np.float32),
        "offs": striped8(idx),
    }


def reference(hid, voc_words, voc_scales, aim, dhid, base, offs):
    idx = unstriped8(offs)
    vocu = unpack_weight(voc_words, voc_scales, "e2m1")
    hidq = mxq(f64(hid), 0, "e4m3")
    a = hidq.T @ vocu
    dhidq = mxq(f64(dhid), 0, "e4m3")
    ta = dhidq.T @ vocu
    m1 = np.max(a, axis=1, keepdims=True)
    lx = pick8(a, idx, 16) - m1
    px = np.exp(lx)
    zl = np.sum(px, axis=1, keepdims=True)
    et = np.log(zl) - np.sum(px * lx, axis=1, keepdims=True) / zl
    det = (et - f64(aim)) * 2.0
    dzl = det / zl - det * (-1.0) * np.sum(px * lx, axis=1, keepdims=True) / np.square(zl)
    dpx = det * (-1.0) / zl * lx + dzl
    xlx = pick8(ta, idx, 16)
    xpx = xlx * px
    xzl = np.sum(xpx, axis=1, keepdims=True)
    xet = xzl / zl - (np.sum(xpx * lx + xlx * px, axis=1, keepdims=True) - xzl * np.sum(px * lx, axis=1, keepdims=True) / zl) / zl
    xdet = xet * 2.0
    xdzl = (xdet - xzl * det / zl) / zl - (xdet * (-1.0) * np.sum(px * lx, axis=1, keepdims=True) + np.sum(xpx * lx + xlx * px, axis=1, keepdims=True) * det * (-1.0) - xzl * zl * 2.0 * det * (-1.0) * np.sum(px * lx, axis=1, keepdims=True) / np.square(zl)) / np.square(zl)
    xdpx = (xdet * (-1.0) - xzl * det * (-1.0) / zl) / zl * lx + xlx * det * (-1.0) / zl + xdzl
    xdlx = (xdet * (-1.0) - xzl * det * (-1.0) / zl) / zl * px + xpx * det * (-1.0) / zl + xdpx * px + xpx * dpx
    xs1 = np.zeros((Q, V))
    xs1[np.arange(Q)[:, None], idx[np.arange(Q) % 128 // 16]] = xdlx
    y = xs1 * 256.0 + f64(base)
    return y

@@ -1,0 +1,173 @@
+from contextlib import ExitStack
+
+import concourse.mybir as mybir
+
+D, V, Q, LISTED = 512, 2048, 128, 512
+FLOPS = 2 * 2 * D * Q * V
+
+F32 = mybir.dt.float32
+BF16 = mybir.dt.bfloat16
+I32 = mybir.dt.int32
+U32 = mybir.dt.uint32
+U16 = mybir.dt.uint16
+U8 = mybir.dt.uint8
+FP8X4 = mybir.dt.float8_e4m3fn_x4
+FP4X4 = mybir.dt.float4_e2m1fn_x4
+ALU = mybir.AluOpType
+ACT = mybir.ActivationFunctionType
+AXIS = mybir.AxisListType
+
+P = 128
+PACK = 4
+BANK = 512
+BANKS = V // BANK
+WORD_LOADS = ((0, 512), (512, 1024), (1024, 2048))
+STORE = 256
+
+
+def tile_attend_hvlistspread_heads_kernel(tc, hid, voc_words, voc_scales, aim, dhid, base, offs, out):
+    nc = tc.nc
+    with ExitStack() as ctx:
+        sb = ctx.enter_context(tc.tile_pool(name="sb", bufs=1))
+        psum = ctx.enter_context(tc.psum_pool(name="psum", bufs=1))
+
+        def column(name):
+            return sb.tile([P, 1], F32, name=name)
+
+        offsets = sb.tile([P, LISTED // 16], U16, name="offsets")
+        hid_raw = sb.tile([P, PACK, Q], F32, name="hid_raw")
+        dhid_raw = sb.tile([P, PACK, Q], F32, name="dhid_raw")
+        voc_plane = sb.tile([P, V], U8, name="voc_plane", align_bytes=64)
+        words = [sb.tile([P, 2 * (hi - lo)], U8, name=f"words{lo}", align_bytes=64) for lo, hi in WORD_LOADS]
+        aim_col = column("aim_col")
+        base_sb = sb.tile([P, V], F32, name="base_sb")
+        window = sb.tile([P, V], F32, name="window")
+
+        nc.vector.memset(voc_plane[:].bitcast(I32), 0)
+        nc.sync.dma_start(out=hid_raw[:], in_=hid.rearrange("(p j) q -> p j q", j=PACK))
+        for quad in range(4):
+            nc.sync.dma_start(
+                out=voc_plane[32 * quad : 32 * quad + 4, :].bitcast(I32),
+                in_=voc_scales[0, 4 * quad : 4 * quad + 4, :].bitcast(I32),
+            )
+
+        def load_words(h):
+            lo, hi = WORD_LOADS[h]
+            nc.sync.dma_start(out=words[h][:].bitcast(I32), in_=voc_words[0, :, 2 * lo : 2 * hi].bitcast(I32))
+
+        load_words(0)
+        load_words(1)
+        nc.sync.dma_start(out=dhid_raw[:], in_=dhid.rearrange("(p j) q -> p j q", j=PACK))
+        load_words(2)
+        nc.sync.dma_start(offsets[:], offs)
+        nc.sync.dma_start(out=aim_col[:], in_=aim)
+        nc.sync.dma_start(out=base_sb[:], in_=base)
+        nc.vector.memset(window[:], 0.0)
+
+        def quantise(name, grouped):
+            codes = sb.tile([P, Q], U32, name=name + "_codes", align_bytes=64)
+            plane = sb.tile([P, Q], U8, name=name + "_plane", align_bytes=64)
+            nc.vector.quantize_mx(
+                out=codes[:].bitcast(FP8X4), scales=plane[:], in_=grouped[:].rearrange("p q j -> p (q j)")
+            )
+            return codes, plane
+
+        hid_bf = sb.tile([P, Q, PACK], BF16, name="hid_bf", align_bytes=64)
+        dhid_bf = sb.tile([P, Q, PACK], BF16, name="dhid_bf", tag="late", align_bytes=64)
+        nc.vector.tensor_copy(out=hid_bf[:], in_=hid_raw[:].rearrange("p j q -> p q j"))
+        hid_mx = quantise("hid", hid_bf)
+        nc.scalar.activation(dhid_bf[:], dhid_raw[:].rearrange("p j q -> p q j"), ACT.Copy)
+        dhid_mx = quantise("dhid", dhid_bf)
+
+        def scores(name, operand, b):
+            codes, plane = operand
+            acc = psum.tile([P, BANK], F32, name=f"{name}{b}")
+            h = min(b, len(WORD_LOADS) - 1)
+            c = b * BANK - WORD_LOADS[h][0]
+            nc.tensor.matmul_mx(
+                out=acc[:],
+                lhsT=codes[:].bitcast(FP8X4),
+                lhsT_scale=plane[:],
+                rhs=words[h][:, 2 * c : 2 * (c + BANK)].bitcast(FP4X4),
+                rhs_scale=voc_plane[:, b * BANK : (b + 1) * BANK],
+                start=True,
+                stop=True,
+            )
+            return acc
+
+        a = sb.tile([P, V], F32, name="a")
+        ta = sb.tile([P, V], F32, name="ta")
+        early_max = sb.tile([P, 2], F32, name="early_max")
+        late_max = sb.tile([P, 2], F32, name="late_max", tag="late", align_bytes=64)
+        for b in range(BANKS):
+            acc = scores("a_acc", hid_mx, b)
+            start, top_b = (None, early_max) if b < 2 else (early_max[:, b - 2 : b - 1], late_max)
+            nc.vector.tensor_scalar(
+                a[:, b * BANK : (b + 1) * BANK], acc[:], 1.0, start, ALU.mult, ALU.max, accum_out=top_b[:, b % 2 : b % 2 + 1]
+            )
+        ta_acc = [scores("ta_acc", dhid_mx, b) for b in range(BANKS)]
+
+        def listed(name):
+            return sb.tile([P, LISTED], F32, name=name)
+
+        ga = listed("ga")
+        nc.vector.tensor_copy(ga[:], a[:].indirect(offsets[:]))
+        neg_top = column("neg_top")
+        nc.vector.tensor_reduce(neg_top[:], late_max[:], AXIS.X, ALU.max, negate=True)
+        for b in range(BANKS - 1):
+            nc.scalar.activation(ta[:, b * BANK : (b + 1) * BANK], ta_acc[b][:], ACT.Copy)
+        p = listed("p")
+        z = column("z")
+        nc.scalar.activation(p[:], ga[:], ACT.Exp, bias=neg_top[:], accum_out=z[:])
+        log_z = column("log_z")
+        nc.scalar.activation(log_z[:], z[:], ACT.Ln)
+        top = column("top")
+        nc.gpsimd.tensor_scalar(top[:], neg_top[:], -1.0, 0.0, ALU.mult, ALU.add)
+
+        nc.vector.tensor_copy(ta[:, (BANKS - 1) * BANK :], ta_acc[BANKS - 1][:])
+        x = listed("x")
+        nc.vector.tensor_copy(x[:], ta[:].indirect(offsets[:]))
+        rz = column("rz")
+        nc.vector.reciprocal(rz[:], z[:])
+        pl = listed("pl")
+        s1 = column("s1")
+        nc.vector.scalar_tensor_tensor(pl[:], ga[:], neg_top[:], p[:], ALU.add, ALU.mult, accum_out=s1[:])
+        xq = listed("xq")
+        x_mean = column("x_mean")
+        nc.vector.scalar_tensor_tensor(xq[:], x[:], rz[:], p[:], ALU.mult, ALU.mult, accum_out=x_mean[:])
+
+        a_mean = column("a_mean")
+        nc.scalar.activation(a_mean[:], s1[:], ACT.Identity, scale=rz[:], bias=top[:])
+        shifted_aim = column("shifted_aim")
+        nc.scalar.activation(shifted_aim[:], s1[:], ACT.Identity, scale=rz[:], bias=aim_col[:])
+        neg_gap = column("neg_gap")
+        nc.scalar.activation(neg_gap[:], log_z[:], ACT.Identity, scale=-1.0, bias=shifted_aim[:])
+        one_less_mean = column("one_less_mean")
+        nc.scalar.activation(one_less_mean[:], a_mean[:], ACT.Copy, scale=-1.0, bias=1.0)
+        f_bias = column("f_bias")
+        nc.scalar.activation(f_bias[:], one_less_mean[:], ACT.Copy, scale=neg_gap[:])
+        g_bias = column("g_bias")
+        nc.scalar.activation(g_bias[:], a_mean[:], ACT.Identity, bias=neg_gap[:])
+        f = listed("f")
+        nc.scalar.activation(f[:], ga[:], ACT.Identity, scale=neg_gap[:], bias=f_bias[:])
+        g = listed("g")
+        nc.scalar.activation(g[:], ga[:], ACT.Identity, scale=-1.0, bias=g_bias[:])
+        row_scale = column("row_scale")
+        nc.gpsimd.tensor_scalar(row_scale[:], rz[:], -512.0, 0.0, ALU.mult, ALU.add)
+
+        xql = listed("xql")
+        cov = column("cov")
+        nc.vector.scalar_tensor_tensor(xql[:], ga[:], a_mean[:], xq[:], ALU.subtract, ALU.mult, accum_out=cov[:])
+        xf = listed("xf")
+        nc.vector.scalar_tensor_tensor(xf[:], x[:], x_mean[:], f[:], ALU.subtract, ALU.mult)
+        w = listed("w")
+        nc.vector.scalar_tensor_tensor(w[:], g[:], cov[:], xf[:], ALU.mult, ALU.subtract)
+        nc.vector.tensor_tensor(window[:].indirect(offsets[:]), w[:], p[:], ALU.mult)
+
+        result = sb.tile([P, V], F32, name="result")
+        for i in range(V // STORE):
+            cols = slice(i * STORE, (i + 1) * STORE)
+            nc.vector.scalar_tensor_tensor(
+                result[:, cols], window[:, cols], row_scale[:], base_sb[:, cols], ALU.mult, ALU.add
+            )
+            nc.sync.dma_start(out=out[:, cols], in_=result[:, cols])

@@ -20,9 +20,8 @@ AXIS = mybir.AxisListType
 P = 128
 PACK = 4
 BANK = 512
-BANKS = V // BANK
-WORD_LOADS = ((0, 512), (512, 1024), (1024, 2048))
-STORE = 256
+WORD_LOADS = ((0, 1024), (1024, 2048))
+STORES = (256, 256, 512, 512, 256, 256)
 
 
 def tile_attend_hvlistspread_heads_kernel(tc, hid, voc_words, voc_scales, aim, dhid, base, offs, out):
@@ -34,6 +33,9 @@ def tile_attend_hvlistspread_heads_kernel(tc, hid, voc_words, voc_scales, aim, d
         def column(name):
             return sb.tile([P, 1], F32, name=name)
 
+        def listed(name):
+            return sb.tile([P, LISTED], F32, name=name)
+
         offsets = sb.tile([P, LISTED // 16], U16, name="offsets")
         hid_raw = sb.tile([P, PACK, Q], F32, name="hid_raw")
         dhid_raw = sb.tile([P, PACK, Q], F32, name="dhid_raw")
@@ -43,6 +45,10 @@ def tile_attend_hvlistspread_heads_kernel(tc, hid, voc_words, voc_scales, aim, d
         base_sb = sb.tile([P, V], F32, name="base_sb")
         window = sb.tile([P, V], F32, name="window")
 
+        def load_words(h):
+            lo, hi = WORD_LOADS[h]
+            nc.sync.dma_start(out=words[h][:].bitcast(I32), in_=voc_words[0, :, 2 * lo : 2 * hi].bitcast(I32))
+
         nc.vector.memset(voc_plane[:].bitcast(I32), 0)
         nc.sync.dma_start(out=hid_raw[:], in_=hid.rearrange("(p j) q -> p j q", j=PACK))
         for quad in range(4):
@@ -50,21 +56,19 @@ def tile_attend_hvlistspread_heads_kernel(tc, hid, voc_words, voc_scales, aim, d
                 out=voc_plane[32 * quad : 32 * quad + 4, :].bitcast(I32),
                 in_=voc_scales[0, 4 * quad : 4 * quad + 4, :].bitcast(I32),
             )
-
-        def load_words(h):
-            lo, hi = WORD_LOADS[h]
-            nc.sync.dma_start(out=words[h][:].bitcast(I32), in_=voc_words[0, :, 2 * lo : 2 * hi].bitcast(I32))
-
         load_words(0)
-        load_words(1)
         nc.sync.dma_start(out=dhid_raw[:], in_=dhid.rearrange("(p j) q -> p j q", j=PACK))
-        load_words(2)
+        load_words(1)
         nc.sync.dma_start(offsets[:], offs)
         nc.sync.dma_start(out=aim_col[:], in_=aim)
         nc.sync.dma_start(out=base_sb[:], in_=base)
         nc.vector.memset(window[:], 0.0)
 
-        def quantise(name, grouped):
+        def quantise(name, raw):
+            grouped = sb.tile([P, Q, PACK], BF16, name=name + "_bf", tag=name + "_bf", align_bytes=64)
+            woven = raw[:].rearrange("p j q -> p q j")
+            nc.vector.tensor_copy(out=grouped[:, : Q // 2, :], in_=woven[:, : Q // 2, :])
+            nc.scalar.activation(grouped[:, Q // 2 :, :], woven[:, Q // 2 :, :], ACT.Copy)
             codes = sb.tile([P, Q], U32, name=name + "_codes", align_bytes=64)
             plane = sb.tile([P, Q], U8, name=name + "_plane", align_bytes=64)
             nc.vector.quantize_mx(
@@ -72,102 +76,105 @@ def tile_attend_hvlistspread_heads_kernel(tc, hid, voc_words, voc_scales, aim, d
             )
             return codes, plane
 
-        hid_bf = sb.tile([P, Q, PACK], BF16, name="hid_bf", align_bytes=64)
-        dhid_bf = sb.tile([P, Q, PACK], BF16, name="dhid_bf", tag="late", align_bytes=64)
-        nc.vector.tensor_copy(out=hid_bf[:], in_=hid_raw[:].rearrange("p j q -> p q j"))
-        hid_mx = quantise("hid", hid_bf)
-        nc.scalar.activation(dhid_bf[:], dhid_raw[:].rearrange("p j q -> p q j"), ACT.Copy)
-        dhid_mx = quantise("dhid", dhid_bf)
+        hid_mx = quantise("hid", hid_raw)
+        dhid_mx = quantise("dhid", dhid_raw)
 
-        def scores(name, operand, b):
+        def scores(operand, lo, hi, bank):
             codes, plane = operand
-            acc = psum.tile([P, BANK], F32, name=f"{name}{b}")
-            h = min(b, len(WORD_LOADS) - 1)
-            c = b * BANK - WORD_LOADS[h][0]
+            acc = psum.tile([P, hi - lo], F32, name=f"acc{bank}", tag=f"bank{bank}")
+            h = max(i for i, (first, last) in enumerate(WORD_LOADS) if first <= lo)
+            first = WORD_LOADS[h][0]
             nc.tensor.matmul_mx(
                 out=acc[:],
                 lhsT=codes[:].bitcast(FP8X4),
                 lhsT_scale=plane[:],
-                rhs=words[h][:, 2 * c : 2 * (c + BANK)].bitcast(FP4X4),
-                rhs_scale=voc_plane[:, b * BANK : (b + 1) * BANK],
+                rhs=words[h][:, 2 * (lo - first) : 2 * (hi - first)].bitcast(FP4X4),
+                rhs_scale=voc_plane[:, lo:hi],
                 start=True,
                 stop=True,
             )
             return acc
 
-        a = sb.tile([P, V], F32, name="a")
-        ta = sb.tile([P, V], F32, name="ta")
-        early_max = sb.tile([P, 2], F32, name="early_max")
-        late_max = sb.tile([P, 2], F32, name="late_max", tag="late", align_bytes=64)
-        for b in range(BANKS):
-            acc = scores("a_acc", hid_mx, b)
-            start, top_b = (None, early_max) if b < 2 else (early_max[:, b - 2 : b - 1], late_max)
-            nc.vector.tensor_scalar(
-                a[:, b * BANK : (b + 1) * BANK], acc[:], 1.0, start, ALU.mult, ALU.max, accum_out=top_b[:, b % 2 : b % 2 + 1]
-            )
-        ta_acc = [scores("ta_acc", dhid_mx, b) for b in range(BANKS)]
+        def on_scalar(dst, acc):
+            nc.scalar.activation(dst, acc[:], ACT.Copy)
 
-        def listed(name):
-            return sb.tile([P, LISTED], F32, name=name)
+        def on_vector(dst, acc):
+            nc.vector.tensor_copy(dst, acc[:])
+
+        a = sb.tile([P, V], F32, name="a", tag="dhid_bf", align_bytes=64)
+        ta = sb.tile([P, V], F32, name="ta")
+        a_parts = (
+            (0, 512, on_vector),
+            (512, 1024, on_scalar),
+            (1024, 1536, on_vector),
+            (1536, 1792, on_scalar),
+            (1792, 2048, on_vector),
+        )
+        for bank, (lo, hi, empty) in enumerate(a_parts):
+            empty(a[:, lo:hi], scores(hid_mx, lo, hi, bank))
+        ta_parts = ((0, 512), (512, 1024), (1024, 1536), (1536, 1792), (1792, 2048))
+        ta_acc = [scores(dhid_mx, lo, hi, bank) for (lo, hi), bank in zip(ta_parts, (5, 6, 7, 3, 4))]
 
         ga = listed("ga")
         nc.vector.tensor_copy(ga[:], a[:].indirect(offsets[:]))
         neg_top = column("neg_top")
-        nc.vector.tensor_reduce(neg_top[:], late_max[:], AXIS.X, ALU.max, negate=True)
-        for b in range(BANKS - 1):
-            nc.scalar.activation(ta[:, b * BANK : (b + 1) * BANK], ta_acc[b][:], ACT.Copy)
+        nc.vector.tensor_reduce(neg_top[:], ga[:], AXIS.X, ALU.max, negate=True)
+        for (lo, hi), acc in list(zip(ta_parts, ta_acc))[:-1]:
+            on_scalar(ta[:, lo:hi], acc)
         p = listed("p")
         z = column("z")
         nc.scalar.activation(p[:], ga[:], ACT.Exp, bias=neg_top[:], accum_out=z[:])
         log_z = column("log_z")
         nc.scalar.activation(log_z[:], z[:], ACT.Ln)
-        top = column("top")
-        nc.gpsimd.tensor_scalar(top[:], neg_top[:], -1.0, 0.0, ALU.mult, ALU.add)
 
-        nc.vector.tensor_copy(ta[:, (BANKS - 1) * BANK :], ta_acc[BANKS - 1][:])
+        on_vector(ta[:, ta_parts[-1][0] :], ta_acc[-1])
         x = listed("x")
         nc.vector.tensor_copy(x[:], ta[:].indirect(offsets[:]))
         rz = column("rz")
         nc.vector.reciprocal(rz[:], z[:])
-        pl = listed("pl")
-        s1 = column("s1")
-        nc.vector.scalar_tensor_tensor(pl[:], ga[:], neg_top[:], p[:], ALU.add, ALU.mult, accum_out=s1[:])
+        pa = listed("pa")
+        a_sum = column("a_sum")
+        nc.vector.scalar_tensor_tensor(pa[:], ga[:], 1.0, p[:], ALU.mult, ALU.mult, accum_out=a_sum[:])
         xq = listed("xq")
         x_mean = column("x_mean")
         nc.vector.scalar_tensor_tensor(xq[:], x[:], rz[:], p[:], ALU.mult, ALU.mult, accum_out=x_mean[:])
+        xqa = listed("xqa")
+        xa_mean = column("xa_mean")
+        nc.vector.scalar_tensor_tensor(xqa[:], x[:], rz[:], pa[:], ALU.mult, ALU.mult, accum_out=xa_mean[:])
 
-        a_mean = column("a_mean")
-        nc.scalar.activation(a_mean[:], s1[:], ACT.Identity, scale=rz[:], bias=top[:])
-        shifted_aim = column("shifted_aim")
-        nc.scalar.activation(shifted_aim[:], s1[:], ACT.Identity, scale=rz[:], bias=aim_col[:])
+        aim_less_top = column("aim_less_top")
+        nc.scalar.activation(aim_less_top[:], neg_top[:], ACT.Identity, bias=aim_col[:])
+        gap_start = column("gap_start")
+        nc.scalar.activation(gap_start[:], a_sum[:], ACT.Identity, scale=rz[:], bias=aim_less_top[:])
+        mean_less_one = column("mean_less_one")
+        nc.scalar.activation(mean_less_one[:], a_sum[:], ACT.Copy, scale=rz[:], bias=-1.0)
         neg_gap = column("neg_gap")
-        nc.scalar.activation(neg_gap[:], log_z[:], ACT.Identity, scale=-1.0, bias=shifted_aim[:])
-        one_less_mean = column("one_less_mean")
-        nc.scalar.activation(one_less_mean[:], a_mean[:], ACT.Copy, scale=-1.0, bias=1.0)
-        f_bias = column("f_bias")
-        nc.scalar.activation(f_bias[:], one_less_mean[:], ACT.Copy, scale=neg_gap[:])
-        g_bias = column("g_bias")
-        nc.scalar.activation(g_bias[:], a_mean[:], ACT.Identity, bias=neg_gap[:])
-        f = listed("f")
-        nc.scalar.activation(f[:], ga[:], ACT.Identity, scale=neg_gap[:], bias=f_bias[:])
+        nc.scalar.activation(neg_gap[:], log_z[:], ACT.Identity, scale=-1.0, bias=gap_start[:])
+        a_mean = column("a_mean")
+        nc.scalar.activation(a_mean[:], a_sum[:], ACT.Copy, scale=rz[:])
+        g_bias = sb.tile([P, 1], F32, name="g_bias", tag="g_bias")
+        nc.scalar.activation(g_bias[:], a_sum[:], ACT.Identity, scale=rz[:], bias=neg_gap[:])
         g = listed("g")
         nc.scalar.activation(g[:], ga[:], ACT.Identity, scale=-1.0, bias=g_bias[:])
         row_scale = column("row_scale")
-        nc.gpsimd.tensor_scalar(row_scale[:], rz[:], -512.0, 0.0, ALU.mult, ALU.add)
+        nc.scalar.activation(row_scale[:], rz[:], ACT.Copy, scale=512.0)
+        pk = sb.tile([P, LISTED], F32, name="pk", tag="g_bias")
+        nc.scalar.activation(pk[:], p[:], ACT.Copy, scale=row_scale[:])
 
-        xql = listed("xql")
-        cov = column("cov")
-        nc.vector.scalar_tensor_tensor(xql[:], ga[:], a_mean[:], xq[:], ALU.subtract, ALU.mult, accum_out=cov[:])
+        f = listed("f")
+        nc.vector.tensor_scalar(f[:], ga[:], mean_less_one[:], neg_gap[:], ALU.subtract, ALU.mult)
+        neg_cov = column("neg_cov")
+        nc.vector.tensor_scalar(neg_cov[:], x_mean[:], a_mean[:], xa_mean[:], ALU.mult, ALU.subtract)
         xf = listed("xf")
         nc.vector.scalar_tensor_tensor(xf[:], x[:], x_mean[:], f[:], ALU.subtract, ALU.mult)
         w = listed("w")
-        nc.vector.scalar_tensor_tensor(w[:], g[:], cov[:], xf[:], ALU.mult, ALU.subtract)
-        nc.vector.tensor_tensor(window[:].indirect(offsets[:]), w[:], p[:], ALU.mult)
+        nc.vector.scalar_tensor_tensor(w[:], g[:], neg_cov[:], xf[:], ALU.mult, ALU.add)
+        nc.vector.tensor_tensor(window[:].indirect(offsets[:]), w[:], pk[:], ALU.mult)
 
         result = sb.tile([P, V], F32, name="result")
-        for i in range(V // STORE):
-            cols = slice(i * STORE, (i + 1) * STORE)
-            nc.vector.scalar_tensor_tensor(
-                result[:, cols], window[:, cols], row_scale[:], base_sb[:, cols], ALU.mult, ALU.add
-            )
+        lo = 0
+        for width in STORES:
+            cols = slice(lo, lo + width)
+            nc.vector.tensor_tensor(result[:, cols], window[:, cols], base_sb[:, cols], ALU.add)
             nc.sync.dma_start(out=out[:, cols], in_=result[:, cols])
+            lo = lo + width

@@ -19,9 +19,11 @@ AXIS = mybir.AxisListType
 
 P = 128
 PACK = 4
-BANK = 512
 WORD_LOADS = ((0, 1024), (1024, 2048))
-STORES = (256, 256, 512, 512, 256, 256)
+PASSES = ((0, 512), (512, 1024), (1024, 1536), (1536, 1792), (1792, 2048))
+A_BANKS = (0, 1, 2, 3, 4)
+TA_BANKS = (5, 6, 7, 3, 4)
+STORES = (256,) * 8
 
 
 def tile_attend_hvlistspread_heads_kernel(tc, hid, voc_words, voc_scales, aim, dhid, base, offs, out):
@@ -39,7 +41,7 @@ def tile_attend_hvlistspread_heads_kernel(tc, hid, voc_words, voc_scales, aim, d
         offsets = sb.tile([P, LISTED // 16], U16, name="offsets")
         hid_raw = sb.tile([P, PACK, Q], F32, name="hid_raw")
         dhid_raw = sb.tile([P, PACK, Q], F32, name="dhid_raw")
-        voc_plane = sb.tile([P, V], U8, name="voc_plane", align_bytes=64)
+        voc_scale_tile = sb.tile([P, V], U8, name="voc_scale_tile", align_bytes=64)
         words = [sb.tile([P, 2 * (hi - lo)], U8, name=f"words{lo}", align_bytes=64) for lo, hi in WORD_LOADS]
         aim_col = column("aim_col")
         base_sb = sb.tile([P, V], F32, name="base_sb")
@@ -49,11 +51,11 @@ def tile_attend_hvlistspread_heads_kernel(tc, hid, voc_words, voc_scales, aim, d
             lo, hi = WORD_LOADS[h]
             nc.sync.dma_start(out=words[h][:].bitcast(I32), in_=voc_words[0, :, 2 * lo : 2 * hi].bitcast(I32))
 
-        nc.vector.memset(voc_plane[:].bitcast(I32), 0)
+        nc.vector.memset(voc_scale_tile[:].bitcast(I32), 0)
         nc.sync.dma_start(out=hid_raw[:], in_=hid.rearrange("(p j) q -> p j q", j=PACK))
         for quad in range(4):
             nc.sync.dma_start(
-                out=voc_plane[32 * quad : 32 * quad + 4, :].bitcast(I32),
+                out=voc_scale_tile[32 * quad : 32 * quad + 4, :].bitcast(I32),
                 in_=voc_scales[0, 4 * quad : 4 * quad + 4, :].bitcast(I32),
             )
         load_words(0)
@@ -70,26 +72,26 @@ def tile_attend_hvlistspread_heads_kernel(tc, hid, voc_words, voc_scales, aim, d
             nc.vector.tensor_copy(out=grouped[:, : Q // 2, :], in_=woven[:, : Q // 2, :])
             nc.scalar.activation(grouped[:, Q // 2 :, :], woven[:, Q // 2 :, :], ACT.Copy)
             codes = sb.tile([P, Q], U32, name=name + "_codes", align_bytes=64)
-            plane = sb.tile([P, Q], U8, name=name + "_plane", align_bytes=64)
+            scale_tile = sb.tile([P, Q], U8, name=name + "_scale_tile", align_bytes=64)
             nc.vector.quantize_mx(
-                out=codes[:].bitcast(FP8X4), scales=plane[:], in_=grouped[:].rearrange("p q j -> p (q j)")
+                out=codes[:].bitcast(FP8X4), scales=scale_tile[:], in_=grouped[:].rearrange("p q j -> p (q j)")
             )
-            return codes, plane
+            return codes, scale_tile
 
         hid_mx = quantise("hid", hid_raw)
         dhid_mx = quantise("dhid", dhid_raw)
 
         def scores(operand, lo, hi, bank):
-            codes, plane = operand
+            codes, scale_tile = operand
             acc = psum.tile([P, hi - lo], F32, name=f"acc{bank}", tag=f"bank{bank}")
             h = max(i for i, (first, last) in enumerate(WORD_LOADS) if first <= lo)
             first = WORD_LOADS[h][0]
             nc.tensor.matmul_mx(
                 out=acc[:],
                 lhsT=codes[:].bitcast(FP8X4),
-                lhsT_scale=plane[:],
+                lhsT_scale=scale_tile[:],
                 rhs=words[h][:, 2 * (lo - first) : 2 * (hi - first)].bitcast(FP4X4),
-                rhs_scale=voc_plane[:, lo:hi],
+                rhs_scale=voc_scale_tile[:, lo:hi],
                 start=True,
                 stop=True,
             )
@@ -103,73 +105,68 @@ def tile_attend_hvlistspread_heads_kernel(tc, hid, voc_words, voc_scales, aim, d
 
         a = sb.tile([P, V], F32, name="a", tag="dhid_bf", align_bytes=64)
         ta = sb.tile([P, V], F32, name="ta")
-        a_parts = (
-            (0, 512, on_vector),
-            (512, 1024, on_scalar),
-            (1024, 1536, on_vector),
-            (1536, 1792, on_scalar),
-            (1792, 2048, on_vector),
-        )
-        for bank, (lo, hi, empty) in enumerate(a_parts):
+        for i, ((lo, hi), bank) in enumerate(zip(PASSES, A_BANKS)):
+            empty = on_scalar if i % 2 else on_vector
             empty(a[:, lo:hi], scores(hid_mx, lo, hi, bank))
-        ta_parts = ((0, 512), (512, 1024), (1024, 1536), (1536, 1792), (1792, 2048))
-        ta_acc = [scores(dhid_mx, lo, hi, bank) for (lo, hi), bank in zip(ta_parts, (5, 6, 7, 3, 4))]
+        ta_acc = [scores(dhid_mx, lo, hi, bank) for (lo, hi), bank in zip(PASSES, TA_BANKS)]
 
-        ga = listed("ga")
-        nc.vector.tensor_copy(ga[:], a[:].indirect(offsets[:]))
+        la = listed("la")
+        nc.vector.tensor_copy(la[:], a[:].indirect(offsets[:]))
         neg_top = column("neg_top")
-        nc.vector.tensor_reduce(neg_top[:], ga[:], AXIS.X, ALU.max, negate=True)
-        for (lo, hi), acc in list(zip(ta_parts, ta_acc))[:-1]:
+        nc.vector.tensor_reduce(neg_top[:], la[:], AXIS.X, ALU.max, negate=True)
+        for (lo, hi), acc in list(zip(PASSES, ta_acc))[:-1]:
             on_scalar(ta[:, lo:hi], acc)
         p = listed("p")
         z = column("z")
-        nc.scalar.activation(p[:], ga[:], ACT.Exp, bias=neg_top[:], accum_out=z[:])
+        nc.scalar.activation(p[:], la[:], ACT.Exp, bias=neg_top[:], accum_out=z[:])
         log_z = column("log_z")
         nc.scalar.activation(log_z[:], z[:], ACT.Ln)
 
-        on_vector(ta[:, ta_parts[-1][0] :], ta_acc[-1])
+        on_vector(ta[:, PASSES[-1][0] :], ta_acc[-1])
         x = listed("x")
         nc.vector.tensor_copy(x[:], ta[:].indirect(offsets[:]))
         rz = column("rz")
         nc.vector.reciprocal(rz[:], z[:])
-        pa = listed("pa")
-        a_sum = column("a_sum")
-        nc.vector.scalar_tensor_tensor(pa[:], ga[:], 1.0, p[:], ALU.mult, ALU.mult, accum_out=a_sum[:])
-        xq = listed("xq")
+        p_la = listed("p_la")
+        la_sum = column("la_sum")
+        nc.vector.scalar_tensor_tensor(p_la[:], la[:], 1.0, p[:], ALU.mult, ALU.mult, accum_out=la_sum[:])
+        x_terms = listed("x_terms")
         x_mean = column("x_mean")
-        nc.vector.scalar_tensor_tensor(xq[:], x[:], rz[:], p[:], ALU.mult, ALU.mult, accum_out=x_mean[:])
-        xqa = listed("xqa")
-        xa_mean = column("xa_mean")
-        nc.vector.scalar_tensor_tensor(xqa[:], x[:], rz[:], pa[:], ALU.mult, ALU.mult, accum_out=xa_mean[:])
+        nc.vector.scalar_tensor_tensor(x_terms[:], x[:], rz[:], p[:], ALU.mult, ALU.mult, accum_out=x_mean[:])
+        x_la_terms = listed("x_la_terms")
+        x_la_mean = column("x_la_mean")
+        nc.vector.scalar_tensor_tensor(
+            x_la_terms[:], x[:], rz[:], p_la[:], ALU.mult, ALU.mult, accum_out=x_la_mean[:]
+        )
 
         aim_less_top = column("aim_less_top")
         nc.scalar.activation(aim_less_top[:], neg_top[:], ACT.Identity, bias=aim_col[:])
-        gap_start = column("gap_start")
-        nc.scalar.activation(gap_start[:], a_sum[:], ACT.Identity, scale=rz[:], bias=aim_less_top[:])
+        neg_gap_plus_log = column("neg_gap_plus_log")
+        nc.scalar.activation(neg_gap_plus_log[:], la_sum[:], ACT.Identity, scale=rz[:], bias=aim_less_top[:])
         mean_less_one = column("mean_less_one")
-        nc.scalar.activation(mean_less_one[:], a_sum[:], ACT.Copy, scale=rz[:], bias=-1.0)
+        nc.scalar.activation(mean_less_one[:], la_sum[:], ACT.Copy, scale=rz[:], bias=-1.0)
         neg_gap = column("neg_gap")
-        nc.scalar.activation(neg_gap[:], log_z[:], ACT.Identity, scale=-1.0, bias=gap_start[:])
-        a_mean = column("a_mean")
-        nc.scalar.activation(a_mean[:], a_sum[:], ACT.Copy, scale=rz[:])
-        g_bias = sb.tile([P, 1], F32, name="g_bias", tag="g_bias")
-        nc.scalar.activation(g_bias[:], a_sum[:], ACT.Identity, scale=rz[:], bias=neg_gap[:])
-        g = listed("g")
-        nc.scalar.activation(g[:], ga[:], ACT.Identity, scale=-1.0, bias=g_bias[:])
+        nc.scalar.activation(neg_gap[:], log_z[:], ACT.Identity, scale=-1.0, bias=neg_gap_plus_log[:])
+        la_mean = column("la_mean")
+        nc.scalar.activation(la_mean[:], la_sum[:], ACT.Copy, scale=rz[:])
+        mean_less_gap = sb.tile([P, 1], F32, name="mean_less_gap", tag="mean_less_gap")
+        nc.scalar.activation(mean_less_gap[:], la_sum[:], ACT.Identity, scale=rz[:], bias=neg_gap[:])
+        cov_factor = listed("cov_factor")
+        nc.scalar.activation(cov_factor[:], la[:], ACT.Identity, scale=-1.0, bias=mean_less_gap[:])
         row_scale = column("row_scale")
         nc.scalar.activation(row_scale[:], rz[:], ACT.Copy, scale=512.0)
-        pk = sb.tile([P, LISTED], F32, name="pk", tag="g_bias")
-        nc.scalar.activation(pk[:], p[:], ACT.Copy, scale=row_scale[:])
+        weights = sb.tile([P, LISTED], F32, name="weights", tag="mean_less_gap")
+        nc.scalar.activation(weights[:], p[:], ACT.Copy, scale=row_scale[:])
 
-        f = listed("f")
-        nc.vector.tensor_scalar(f[:], ga[:], mean_less_one[:], neg_gap[:], ALU.subtract, ALU.mult)
+        x_factor = listed("x_factor")
+        nc.vector.tensor_scalar(x_factor[:], la[:], mean_less_one[:], neg_gap[:], ALU.subtract, ALU.mult)
         neg_cov = column("neg_cov")
-        nc.vector.tensor_scalar(neg_cov[:], x_mean[:], a_mean[:], xa_mean[:], ALU.mult, ALU.subtract)
-        xf = listed("xf")
-        nc.vector.scalar_tensor_tensor(xf[:], x[:], x_mean[:], f[:], ALU.subtract, ALU.mult)
-        w = listed("w")
-        nc.vector.scalar_tensor_tensor(w[:], g[:], neg_cov[:], xf[:], ALU.mult, ALU.add)
-        nc.vector.tensor_tensor(window[:].indirect(offsets[:]), w[:], pk[:], ALU.mult)
+        nc.vector.tensor_scalar(neg_cov[:], x_mean[:], la_mean[:], x_la_mean[:], ALU.mult, ALU.subtract)
+        x_part = listed("x_part")
+        nc.vector.scalar_tensor_tensor(x_part[:], x[:], x_mean[:], x_factor[:], ALU.subtract, ALU.mult)
+        bracket = listed("bracket")
+        nc.vector.scalar_tensor_tensor(bracket[:], cov_factor[:], neg_cov[:], x_part[:], ALU.mult, ALU.add)
+        nc.vector.tensor_tensor(window[:].indirect(offsets[:]), bracket[:], weights[:], ALU.mult)
 
         result = sb.tile([P, V], F32, name="result")
         lo = 0

from contextlib import ExitStack

import concourse.mybir as mybir

D, V, Q, LISTED = 512, 2048, 128, 512
FLOPS = 2 * 2 * D * Q * V

F32 = mybir.dt.float32
BF16 = mybir.dt.bfloat16
I32 = mybir.dt.int32
U32 = mybir.dt.uint32
U16 = mybir.dt.uint16
U8 = mybir.dt.uint8
FP8X4 = mybir.dt.float8_e4m3fn_x4
FP4X4 = mybir.dt.float4_e2m1fn_x4
ALU = mybir.AluOpType
ACT = mybir.ActivationFunctionType
AXIS = mybir.AxisListType

P = 128
PACK = 4
WORD_LOADS = ((0, 1024), (1024, 2048))
PASSES = ((0, 512), (512, 1024), (1024, 1536), (1536, 1792), (1792, 2048))
A_BANKS = (0, 1, 2, 3, 4)
TA_BANKS = (5, 6, 7, 3, 4)
STORES = (256,) * 8


def tile_attend_hvlistspread_heads_kernel(tc, hid, voc_words, voc_scales, aim, dhid, base, offs, out):
    nc = tc.nc
    with ExitStack() as ctx:
        sb = ctx.enter_context(tc.tile_pool(name="sb", bufs=1))
        psum = ctx.enter_context(tc.psum_pool(name="psum", bufs=1))

        def column(name):
            return sb.tile([P, 1], F32, name=name)

        def listed(name):
            return sb.tile([P, LISTED], F32, name=name)

        offsets = sb.tile([P, LISTED // 16], U16, name="offsets")
        hid_raw = sb.tile([P, PACK, Q], F32, name="hid_raw")
        dhid_raw = sb.tile([P, PACK, Q], F32, name="dhid_raw")
        voc_scale_tile = sb.tile([P, V], U8, name="voc_scale_tile", align_bytes=64)
        words = [sb.tile([P, 2 * (hi - lo)], U8, name=f"words{lo}", align_bytes=64) for lo, hi in WORD_LOADS]
        aim_col = column("aim_col")
        base_sb = sb.tile([P, V], F32, name="base_sb")
        window = sb.tile([P, V], F32, name="window")

        def load_words(h):
            lo, hi = WORD_LOADS[h]
            nc.sync.dma_start(out=words[h][:].bitcast(I32), in_=voc_words[0, :, 2 * lo : 2 * hi].bitcast(I32))

        nc.vector.memset(voc_scale_tile[:].bitcast(I32), 0)
        nc.sync.dma_start(out=hid_raw[:], in_=hid.rearrange("(p j) q -> p j q", j=PACK))
        for quad in range(4):
            nc.sync.dma_start(
                out=voc_scale_tile[32 * quad : 32 * quad + 4, :].bitcast(I32),
                in_=voc_scales[0, 4 * quad : 4 * quad + 4, :].bitcast(I32),
            )
        load_words(0)
        nc.sync.dma_start(out=dhid_raw[:], in_=dhid.rearrange("(p j) q -> p j q", j=PACK))
        load_words(1)
        nc.sync.dma_start(offsets[:], offs)
        nc.sync.dma_start(out=aim_col[:], in_=aim)
        nc.sync.dma_start(out=base_sb[:], in_=base)
        nc.vector.memset(window[:], 0.0)

        def quantise(name, raw):
            grouped = sb.tile([P, Q, PACK], BF16, name=name + "_bf", tag=name + "_bf", align_bytes=64)
            woven = raw[:].rearrange("p j q -> p q j")
            nc.vector.tensor_copy(out=grouped[:, : Q // 2, :], in_=woven[:, : Q // 2, :])
            nc.scalar.activation(grouped[:, Q // 2 :, :], woven[:, Q // 2 :, :], ACT.Copy)
            codes = sb.tile([P, Q], U32, name=name + "_codes", align_bytes=64)
            scale_tile = sb.tile([P, Q], U8, name=name + "_scale_tile", align_bytes=64)
            nc.vector.quantize_mx(
                out=codes[:].bitcast(FP8X4), scales=scale_tile[:], in_=grouped[:].rearrange("p q j -> p (q j)")
            )
            return codes, scale_tile

        hid_mx = quantise("hid", hid_raw)
        dhid_mx = quantise("dhid", dhid_raw)

        def scores(operand, lo, hi, bank):
            codes, scale_tile = operand
            acc = psum.tile([P, hi - lo], F32, name=f"acc{bank}", tag=f"bank{bank}")
            h = max(i for i, (first, last) in enumerate(WORD_LOADS) if first <= lo)
            first = WORD_LOADS[h][0]
            nc.tensor.matmul_mx(
                out=acc[:],
                lhsT=codes[:].bitcast(FP8X4),
                lhsT_scale=scale_tile[:],
                rhs=words[h][:, 2 * (lo - first) : 2 * (hi - first)].bitcast(FP4X4),
                rhs_scale=voc_scale_tile[:, lo:hi],
                start=True,
                stop=True,
            )
            return acc

        def on_scalar(dst, acc):
            nc.scalar.activation(dst, acc[:], ACT.Copy)

        def on_vector(dst, acc):
            nc.vector.tensor_copy(dst, acc[:])

        a = sb.tile([P, V], F32, name="a", tag="dhid_bf", align_bytes=64)
        ta = sb.tile([P, V], F32, name="ta")
        for i, ((lo, hi), bank) in enumerate(zip(PASSES, A_BANKS)):
            empty = on_scalar if i % 2 else on_vector
            empty(a[:, lo:hi], scores(hid_mx, lo, hi, bank))
        ta_acc = [scores(dhid_mx, lo, hi, bank) for (lo, hi), bank in zip(PASSES, TA_BANKS)]

        la = listed("la")
        nc.vector.tensor_copy(la[:], a[:].indirect(offsets[:]))
        neg_top = column("neg_top")
        nc.vector.tensor_reduce(neg_top[:], la[:], AXIS.X, ALU.max, negate=True)
        for (lo, hi), acc in list(zip(PASSES, ta_acc))[:-1]:
            on_scalar(ta[:, lo:hi], acc)
        p = listed("p")
        z = column("z")
        nc.scalar.activation(p[:], la[:], ACT.Exp, bias=neg_top[:], accum_out=z[:])
        log_z = column("log_z")
        nc.scalar.activation(log_z[:], z[:], ACT.Ln)

        on_vector(ta[:, PASSES[-1][0] :], ta_acc[-1])
        x = listed("x")
        nc.vector.tensor_copy(x[:], ta[:].indirect(offsets[:]))
        rz = column("rz")
        nc.vector.reciprocal(rz[:], z[:])
        p_la = listed("p_la")
        la_sum = column("la_sum")
        nc.vector.scalar_tensor_tensor(p_la[:], la[:], 1.0, p[:], ALU.mult, ALU.mult, accum_out=la_sum[:])
        x_terms = listed("x_terms")
        x_mean = column("x_mean")
        nc.vector.scalar_tensor_tensor(x_terms[:], x[:], rz[:], p[:], ALU.mult, ALU.mult, accum_out=x_mean[:])
        x_la_terms = listed("x_la_terms")
        x_la_mean = column("x_la_mean")
        nc.vector.scalar_tensor_tensor(
            x_la_terms[:], x[:], rz[:], p_la[:], ALU.mult, ALU.mult, accum_out=x_la_mean[:]
        )

        aim_less_top = column("aim_less_top")
        nc.scalar.activation(aim_less_top[:], neg_top[:], ACT.Identity, bias=aim_col[:])
        neg_gap_plus_log = column("neg_gap_plus_log")
        nc.scalar.activation(neg_gap_plus_log[:], la_sum[:], ACT.Identity, scale=rz[:], bias=aim_less_top[:])
        mean_less_one = column("mean_less_one")
        nc.scalar.activation(mean_less_one[:], la_sum[:], ACT.Copy, scale=rz[:], bias=-1.0)
        neg_gap = column("neg_gap")
        nc.scalar.activation(neg_gap[:], log_z[:], ACT.Identity, scale=-1.0, bias=neg_gap_plus_log[:])
        la_mean = column("la_mean")
        nc.scalar.activation(la_mean[:], la_sum[:], ACT.Copy, scale=rz[:])
        mean_less_gap = sb.tile([P, 1], F32, name="mean_less_gap", tag="mean_less_gap")
        nc.scalar.activation(mean_less_gap[:], la_sum[:], ACT.Identity, scale=rz[:], bias=neg_gap[:])
        cov_factor = listed("cov_factor")
        nc.scalar.activation(cov_factor[:], la[:], ACT.Identity, scale=-1.0, bias=mean_less_gap[:])
        row_scale = column("row_scale")
        nc.scalar.activation(row_scale[:], rz[:], ACT.Copy, scale=512.0)
        weights = sb.tile([P, LISTED], F32, name="weights", tag="mean_less_gap")
        nc.scalar.activation(weights[:], p[:], ACT.Copy, scale=row_scale[:])

        x_factor = listed("x_factor")
        nc.vector.tensor_scalar(x_factor[:], la[:], mean_less_one[:], neg_gap[:], ALU.subtract, ALU.mult)
        neg_cov = column("neg_cov")
        nc.vector.tensor_scalar(neg_cov[:], x_mean[:], la_mean[:], x_la_mean[:], ALU.mult, ALU.subtract)
        x_part = listed("x_part")
        nc.vector.scalar_tensor_tensor(x_part[:], x[:], x_mean[:], x_factor[:], ALU.subtract, ALU.mult)
        bracket = listed("bracket")
        nc.vector.scalar_tensor_tensor(bracket[:], cov_factor[:], neg_cov[:], x_part[:], ALU.mult, ALU.add)
        nc.vector.tensor_tensor(window[:].indirect(offsets[:]), bracket[:], weights[:], ALU.mult)

        result = sb.tile([P, V], F32, name="result")
        lo = 0
        for width in STORES:
            cols = slice(lo, lo + width)
            nc.vector.tensor_tensor(result[:, cols], window[:, cols], base_sb[:, cols], ALU.add)
            nc.sync.dma_start(out=out[:, cols], in_=result[:, cols])
            lo = lo + width
